import numpy as np, ml_dtypes
CORES = [44,45,46,47,172,173,174,175,300,301,302,303,428,429,430,431]
N = 16
T = 256
def entries(a): return a.T.reshape(-1)
def pack(v, P): return np.ascontiguousarray(np.asarray(v, np.int32).reshape(-1, P).T)
def lists(rng, how):
    Q = rng.permutation(N * T)
    if how == "stay": Q = np.arange(N * T)
    if how == "own": Q = np.concatenate([T * r + rng.permutation(T) for r in range(N)])
    if how == "shift": Q = (np.arange(N * T) + T * int(rng.integers(1, N)) + 1) % (N * T)
    if how == "deal": Q = (np.arange(N * T) % N) * T + np.arange(N * T) // N
    if how == "block": s = int(rng.integers(1, N)); Q = np.concatenate([T * ((r + s) % N) + rng.permutation(T) for r in range(N)])
    return {"goes": np.broadcast_to(pack(Q, 16), (N, 16, N * T // 16)).copy()}
def setup_inputs(rng):
    return dict({"x": rng.standard_normal((N, 128, T), dtype=np.float32).astype(ml_dtypes.bfloat16)}, **lists(rng, "uniform"))
def setup_inputs_block(rng):
    d = setup_inputs(rng); d.update(lists(rng, "block"))
    for k in ("x",): d[k] = (d[k].astype(np.float32) * 1048576.0).astype(d[k].dtype)
    return d
def setup_inputs_deal(rng):
    d = setup_inputs(rng); d.update(lists(rng, "deal"))
    for k in ("x",): d[k] = (d[k].astype(np.float32) * (1 / 1024.0)).astype(d[k].dtype)
    return d
def setup_inputs_own(rng):
    d = setup_inputs(rng); d.update(lists(rng, "own"))
    return d
def setup_inputs_shift(rng):
    d = setup_inputs(rng); d.update(lists(rng, "shift"))
    return d
def setup_inputs_stay(rng):
    d = setup_inputs(rng); d.update(lists(rng, "stay"))
    return d
def check_inputs(x):
    bad = []
    if x["goes"].min() < 0 or x["goes"].max() >= N * T: bad.append("goes out of range")
    if not np.array_equal(np.sort(entries(x["goes"][0])), np.arange(N * T)): bad.append("goes isn't a permutation")
    if not all(np.array_equal(a, x["goes"][0]) for a in x["goes"]): bad.append("goes isn't alike on all ranks")
    return bad
def reference(x, goes):
    A = np.concatenate(list(x), axis=1); Y = np.zeros_like(A)
    Y[:, entries(goes[0])] = A
    return {"y": np.stack([Y[:, T * r:T * r + T] for r in range(N)])}

@@ -1,0 +1,206 @@
+from concourse.bass import DstId, RemoteDMATransfer
+from concourse.mybir import AluOpType
+
+SCRATCH = {
+    "A": ("sbuf", [128, 1024], "bfloat16"),
+    "S": ("sbuf", [128, 1024], "bfloat16"),
+    "Lnd": ("sbuf", [128, 1024], "bfloat16"),
+    "Y": ("sbuf", [128, 256], "bfloat16"),
+    "G": ("sbuf", [128, 32], "int32"),
+    "OFFG": ("sbuf", [128, 32], "uint16"),
+    "IV": ("sbuf", [128, 512], "int32"),
+    "VAL": ("sbuf", [128, 512], "int32"),
+    "W": ("sbuf", [128, 4096], "float32"),
+    "IL": ("sbuf", [128, 128], "int32"),
+    "IL2": ("sbuf", [128, 128], "int32"),
+    "L": ("sbuf", [128, 128], "float32"),
+    "IM": ("sbuf", [128, 64], "int32"),
+    "IM2": ("sbuf", [128, 64], "int32"),
+    "Mask": ("sbuf", [128, 64], "float32"),
+    "R": ("sbuf", [128, 64], "float32"),
+    "I": ("sbuf", [128, 64], "int32"),
+    "Hq": ("sbuf", [128, 64], "int32"),
+    "U": ("sbuf", [128, 64], "int32"),
+    "S1": ("sbuf", [128, 64], "int32"),
+    "OFF1": ("sbuf", [128, 64], "uint16"),
+    "X": ("sbuf", [128, 16], "int32"),
+    "XA": ("sbuf", [128, 16], "int32"),
+    "XB": ("sbuf", [128, 16], "int32"),
+    "TP": ("sbuf", [128, 16], "int32"),
+    "K2": ("sbuf", [128, 16], "int32"),
+    "S2": ("sbuf", [128, 16], "int32"),
+    "OFF2": ("sbuf", [128, 16], "uint16"),
+    "P1": ("psum", [128, 512], "float32"),
+    "P2": ("psum", [128, 512], "float32"),
+}
+SEMAPHORES = ["xl", "gl", "gi", "vs", "ts", "tl", "yd", "st", "asw", "acb", "adg", "atl", "snt"]
+
+C = 256
+
+
+def _bits(mask):
+    return [e for e in range(16) if (mask >> e) & 1]
+
+
+def _mask(engines):
+    m = 0
+    for e in engines:
+        m |= 1 << e
+    return m
+
+
+def rank_program(g, core, T, topo):
+    rank = T.rank_of(core)
+    if rank is None:
+        return
+    cores = list(T.cores)
+    sem = T.sem
+    A_ = AluOpType
+
+    def place(c):
+        return (topo.host(c), topo.chip(c))
+    groups = []
+    for c in cores:
+        if place(c) not in groups:
+            groups.append(place(c))
+    members = [[c for c in cores if place(c) == gp] for gp in groups]
+    h = groups.index(place(core))
+    k = members[h].index(core)
+    nsib = len(members[h])
+    assert len(groups) == 4 and nsib == 4 and rank == 4 * h + k
+    h_sw = h_cb = None
+    for hh in range(4):
+        if hh == h:
+            continue
+        peer = members[hh][k]
+        if not topo.may_write(core, peer):
+            continue
+        if topo.same_plane(core, peer):
+            h_sw = hh
+        else:
+            h_cb = hh
+    assert h_sw is not None and h_cb is not None
+
+    def slot(buf, n):
+        return buf[:, C * n:C * (n + 1)]
+
+    def dst(c):
+        rid, pid = topo.addr(c, core)
+        return DstId(rid=rid, pnc=pid)
+
+    v, te = g.vector, g.tensor
+    nv = [0]
+
+    def vdone(ins):
+        ins.then_inc(sem.vs, 1)
+        nv[0] += 1
+
+    def vsync():
+        if nv[0]:
+            v.wait_ge(sem.vs, nv[0])
+
+    g.sync.dma_start(slot(T.A, h), T.x[:, :]).then_inc(sem.xl, 16)
+    g.scalar.dma_start(T.G[:, :], T.goes[:, :]).then_inc(sem.gl, 16)
+
+    g.iota(T.IV[:, :], [[128, 32], [8, 2], [4096, 8]], 0, 1).then_inc(sem.gi, 1)
+    g.iota(T.IL[:, :], [[-1, 128]], 128, 1).then_inc(sem.gi, 1)
+    g.iota(T.IM[:, :], [[0, 8], [-16, 8]], 128, 1).then_inc(sem.gi, 1)
+
+    p_sw, p_cb = members[h_sw][k], members[h_cb][k]
+    e_sw, e_cb = _bits(topo.mask(core, p_sw)), _bits(topo.mask(core, p_cb))
+    m_sw, m_cb = e_sw[0::2], [e for e in e_cb if e not in e_sw[0::2]][:len(e_sw[0::2])]
+    sent = 0
+    g.wait_ge(sem.xl, 16)
+    g.remote_dma_fused([
+        RemoteDMATransfer(dst_ids=[dst(p_sw)], dma_engine_mask=_mask(m_sw), remote_sem=sem.asw,
+                          src=slot(T.A, h), dst=slot(T.A, h)),
+        RemoteDMATransfer(dst_ids=[dst(p_cb)], dma_engine_mask=_mask(m_cb), remote_sem=sem.acb,
+                          src=slot(T.A, h), dst=slot(T.A, h)),
+    ], local_sem=sem.snt)
+    sent += len(m_sw) + len(m_cb)
+    g.iota(T.X[:, :], [[128, 16]], 0, 1).then_inc(sem.gi, 1)
+
+    if k % 2 == 0:
+        g.wait_ge(sem.asw, len(m_sw))
+        src_h, to, eng = h_sw, p_cb, e_cb
+    else:
+        g.wait_ge(sem.acb, len(m_cb))
+        src_h, to, eng = h_cb, p_sw, e_sw
+    rid, pid = topo.addr(to, core)
+    g.remote_dma(slot(T.A, src_h), slot(T.A, src_h), sem.adg, sem.snt, pid, rid, _mask(eng))
+    sent += len(eng)
+    n_dg = len(eng)
+
+    base = 4 * C * h
+    vdone(v.memset(T.W[:, base:base + 4 * C], 0.0))
+    v.wait_ge(sem.gi, 3)
+    vdone(v.tensor_scalar(T.VAL[:, :], T.IV[:, :], 3, None, A_.logical_shift_right))
+    vdone(v.tensor_scalar(T.IL2[:, :], T.IL[:, :], 15, None, A_.bitwise_and))
+    vdone(v.tensor_scalar(T.IM2[:, :], T.IM[:, :], 4, None, A_.logical_shift_right))
+    vsync()
+    vdone(v.tensor_scalar(T.L[:, :], T.IL2[:, :], 0, None, A_.is_equal))
+    vdone(v.tensor_scalar(T.Mask[:, :], T.IM2[:, :], 8, None, A_.is_equal))
+    v.wait_ge(sem.gl, 16)
+    vdone(v.tensor_copy(T.OFFG[:, :], T.G[:, :]))
+    vsync()
+    vdone(v.tensor_copy(T.W[:, 0:4096].indirect(T.OFFG[:, 0:32]), T.VAL[:, :]))
+    te.wait_ge(sem.vs, nv[0])
+    for b in range(8):
+        te.matmul(T.P1[:, 8 * b:8 * b + 8], T.W[:, base + 128 * b:base + 128 * (b + 1)], T.L[:, 0:8],
+                  True, True).then_inc(sem.ts, 1)
+    v.wait_ge(sem.ts, 8)
+    vdone(v.tensor_tensor(T.R[:, :], T.P1[:, 0:64], T.Mask[:, :], A_.mult))
+    te.wait_ge(sem.vs, nv[0])
+    te.matmul(T.P2[:, 0:64], T.L[:, :], T.R[:, :], True, True).then_inc(sem.ts, 1)
+    v.wait_ge(sem.ts, 9)
+    vdone(v.tensor_copy(T.I[:, :], T.P2[:, 0:64]))
+    vsync()
+    vdone(v.tensor_scalar(T.Hq[:, :], T.I[:, :], 2, 768, A_.logical_shift_right, A_.bitwise_and))
+    vdone(v.tensor_scalar(T.U[:, :], T.I[:, :], 255, None, A_.bitwise_and))
+    vsync()
+    vdone(v.tensor_tensor(T.S1[:, :], T.Hq[:, :], T.U[:, :], A_.add))
+    vsync()
+    vdone(v.tensor_copy(T.OFF1[:, :], T.S1[:, :]))
+    vsync()
+
+    v.wait_ge(sem.xl, 16)
+    v.wait_ge(sem.asw, len(m_sw))
+    v.wait_ge(sem.acb, len(m_cb))
+    v.wait_ge(sem.adg, n_dg)
+    order = [(k + j) % nsib for j in range(1, nsib)]
+    n_tl = 0
+    for n, d in enumerate(order):
+        v.tensor_copy(slot(T.S, d), T.A[:, 0:4 * C].indirect(T.OFF1[:, 16 * d:16 * (d + 1)])).then_inc(sem.tl, 1)
+        to = members[h][d]
+        eng = _bits(topo.mask(core, to))
+        rid, pid = topo.addr(to, core)
+        g.wait_ge(sem.tl, n + 1)
+        g.remote_dma(slot(T.Lnd, k), slot(T.S, d), sem.atl, sem.snt, pid, rid, _mask(eng))
+        sent += len(eng)
+        n_tl += len(eng)
+    v.tensor_copy(slot(T.Lnd, k), T.A[:, 0:4 * C].indirect(T.OFF1[:, 16 * k:16 * (k + 1)])).then_inc(sem.tl, 1)
+
+    v.wait_ge(sem.gi, 4)
+    vdone(v.tensor_scalar(T.XA[:, :], T.X[:, :], 15, None, A_.bitwise_and))
+    vdone(v.tensor_scalar(T.XB[:, :], T.X[:, :], 3, 240, A_.logical_shift_right, A_.bitwise_and))
+    vdone(v.tensor_scalar(T.K2[:, :], T.I[:, 16 * k:16 * (k + 1)], 768, None, A_.bitwise_and))
+    vsync()
+    vdone(v.tensor_tensor(T.TP[:, :], T.XA[:, :], T.XB[:, :], A_.add))
+    vsync()
+    vdone(v.tensor_tensor(T.S2[:, :], T.K2[:, :], T.TP[:, :], A_.add))
+    vsync()
+    vdone(v.tensor_copy(T.OFF2[:, :], T.S2[:, :]))
+    vsync()
+
+    v.wait_ge(sem.tl, nsib)
+    v.wait_ge(sem.atl, n_tl)
+    v.tensor_copy(T.Y[:, :], T.Lnd[:, 0:4 * C].indirect(T.OFF2[:, 0:16])).then_inc(sem.yd, 1)
+    g.sync.wait_ge(sem.yd, 1)
+    g.sync.dma_start(T.y[:, :], T.Y[:, :]).then_inc(sem.st, 16)
+
+    g.wait_ge(sem.snt, sent)
+    g.wait_ge(sem.asw, len(m_sw))
+    g.wait_ge(sem.acb, len(m_cb))
+    g.wait_ge(sem.adg, n_dg)
+    g.wait_ge(sem.atl, n_tl)
+    g.wait_ge(sem.st, 16)

@@ -4,7 +4,7 @@ from concourse.mybir import AluOpType
 SCRATCH = {
     "A": ("sbuf", [128, 1024], "bfloat16"),
     "S": ("sbuf", [128, 1024], "bfloat16"),
-    "Lnd": ("sbuf", [128, 1024], "bfloat16"),
+    "Lnd": ("sbuf", [128, 2048], "bfloat16"),
     "Y": ("sbuf", [128, 256], "bfloat16"),
     "G": ("sbuf", [128, 32], "int32"),
     "OFFG": ("sbuf", [128, 32], "uint16"),
@@ -28,25 +28,25 @@ SCRATCH = {
     "XB": ("sbuf", [128, 16], "int32"),
     "TP": ("sbuf", [128, 16], "int32"),
     "K2": ("sbuf", [128, 16], "int32"),
+    "U2": ("sbuf", [128, 16], "int32"),
+    "Hh": ("sbuf", [128, 16], "int32"),
+    "Eq": ("sbuf", [128, 16], "int32"),
+    "D1": ("sbuf", [128, 16], "int32"),
+    "D2": ("sbuf", [128, 16], "int32"),
+    "M2": ("sbuf", [128, 16], "int32"),
+    "B2": ("sbuf", [128, 16], "int32"),
     "S2": ("sbuf", [128, 16], "int32"),
     "OFF2": ("sbuf", [128, 16], "uint16"),
     "P1": ("psum", [128, 512], "float32"),
     "P2": ("psum", [128, 512], "float32"),
 }
-SEMAPHORES = ["xl", "gl", "gi", "vs", "ts", "tl", "yd", "st", "asw", "acb", "adg", "atl", "snt"]
+SEMAPHORES = ["xl", "gl", "gi", "vs", "ts", "tl", "yd", "st", "asw", "acb", "adg", "atl", "ard", "snt"]
 
 C = 256
 
 
 def _bits(mask):
     return [e for e in range(16) if (mask >> e) & 1]
-
-
-def _mask(engines):
-    m = 0
-    for e in engines:
-        m |= 1 << e
-    return m
 
 
 def rank_program(g, core, T, topo):
@@ -68,25 +68,30 @@ def rank_program(g, core, T, topo):
     k = members[h].index(core)
     nsib = len(members[h])
     assert len(groups) == 4 and nsib == 4 and rank == 4 * h + k
-    h_sw = h_cb = None
+    h_sw = h_cb = h_far = None
     for hh in range(4):
         if hh == h:
             continue
         peer = members[hh][k]
         if not topo.may_write(core, peer):
-            continue
-        if topo.same_plane(core, peer):
+            h_far = hh
+        elif topo.same_plane(core, peer):
             h_sw = hh
         else:
             h_cb = hh
-    assert h_sw is not None and h_cb is not None
+    assert h_sw is not None and h_cb is not None and h_far is not None
 
     def slot(buf, n):
         return buf[:, C * n:C * (n + 1)]
 
-    def dst(c):
-        rid, pid = topo.addr(c, core)
-        return DstId(rid=rid, pnc=pid)
+    sent = [0]
+
+    def send(to, out, in_, rsem):
+        rid, pid = topo.addr(to, core)
+        m = topo.mask(core, to)
+        g.remote_dma(out, in_, rsem, sem.snt, pid, rid, m)
+        sent[0] += len(_bits(m))
+        return len(_bits(m))
 
     v, te = g.vector, g.tensor
     nv = [0]
@@ -107,32 +112,25 @@ def rank_program(g, core, T, topo):
     g.iota(T.IM[:, :], [[0, 8], [-16, 8]], 128, 1).then_inc(sem.gi, 1)
 
     p_sw, p_cb = members[h_sw][k], members[h_cb][k]
-    e_sw, e_cb = _bits(topo.mask(core, p_sw)), _bits(topo.mask(core, p_cb))
-    m_sw, m_cb = e_sw[0::2], [e for e in e_cb if e not in e_sw[0::2]][:len(e_sw[0::2])]
-    sent = 0
     g.wait_ge(sem.xl, 16)
-    g.remote_dma_fused([
-        RemoteDMATransfer(dst_ids=[dst(p_sw)], dma_engine_mask=_mask(m_sw), remote_sem=sem.asw,
-                          src=slot(T.A, h), dst=slot(T.A, h)),
-        RemoteDMATransfer(dst_ids=[dst(p_cb)], dma_engine_mask=_mask(m_cb), remote_sem=sem.acb,
-                          src=slot(T.A, h), dst=slot(T.A, h)),
-    ], local_sem=sem.snt)
-    sent += len(m_sw) + len(m_cb)
+    if k % 2 == 0:
+        n_sw = send(p_sw, slot(T.A, h), slot(T.A, h), sem.asw)
+        n_cb = send(p_cb, slot(T.A, h), slot(T.A, h), sem.acb)
+    else:
+        n_cb = send(p_cb, slot(T.A, h), slot(T.A, h), sem.acb)
+        n_sw = send(p_sw, slot(T.A, h), slot(T.A, h), sem.asw)
     g.iota(T.X[:, :], [[128, 16]], 0, 1).then_inc(sem.gi, 1)
 
     if k % 2 == 0:
-        g.wait_ge(sem.asw, len(m_sw))
-        src_h, to, eng = h_sw, p_cb, e_cb
+        g.wait_ge(sem.asw, n_sw)
+        n_dg = send(p_cb, slot(T.Lnd, 4 + k), slot(T.A, h_sw), sem.adg)
     else:
-        g.wait_ge(sem.acb, len(m_cb))
-        src_h, to, eng = h_cb, p_sw, e_sw
-    rid, pid = topo.addr(to, core)
-    g.remote_dma(slot(T.A, src_h), slot(T.A, src_h), sem.adg, sem.snt, pid, rid, _mask(eng))
-    sent += len(eng)
-    n_dg = len(eng)
+        g.wait_ge(sem.acb, n_cb)
+        n_dg = send(p_sw, slot(T.Lnd, 4 + k), slot(T.A, h_cb), sem.adg)
 
     base = 4 * C * h
     vdone(v.memset(T.W[:, base:base + 4 * C], 0.0))
+    vdone(v.memset(slot(T.A, h_far), 0.0))
     v.wait_ge(sem.gi, 3)
     vdone(v.tensor_scalar(T.VAL[:, :], T.IV[:, :], 3, None, A_.logical_shift_right))
     vdone(v.tensor_scalar(T.IL2[:, :], T.IL[:, :], 15, None, A_.bitwise_and))
@@ -164,43 +162,64 @@ def rank_program(g, core, T, topo):
     vsync()
 
     v.wait_ge(sem.xl, 16)
-    v.wait_ge(sem.asw, len(m_sw))
-    v.wait_ge(sem.acb, len(m_cb))
-    v.wait_ge(sem.adg, n_dg)
+    v.wait_ge(sem.asw, n_sw)
+    v.wait_ge(sem.acb, n_cb)
     order = [(k + j) % nsib for j in range(1, nsib)]
     n_tl = 0
     for n, d in enumerate(order):
         v.tensor_copy(slot(T.S, d), T.A[:, 0:4 * C].indirect(T.OFF1[:, 16 * d:16 * (d + 1)])).then_inc(sem.tl, 1)
-        to = members[h][d]
-        eng = _bits(topo.mask(core, to))
-        rid, pid = topo.addr(to, core)
         g.wait_ge(sem.tl, n + 1)
-        g.remote_dma(slot(T.Lnd, k), slot(T.S, d), sem.atl, sem.snt, pid, rid, _mask(eng))
-        sent += len(eng)
-        n_tl += len(eng)
+        n_tl += send(members[h][d], slot(T.Lnd, k), slot(T.S, d), sem.atl)
     v.tensor_copy(slot(T.Lnd, k), T.A[:, 0:4 * C].indirect(T.OFF1[:, 16 * k:16 * (k + 1)])).then_inc(sem.tl, 1)
 
+    m_all = topo.mask(core, members[h][order[0]])
+    ids = []
+    for d in order:
+        m_all &= topo.mask(core, members[h][d])
+        rid, pid = topo.addr(members[h][d], core)
+        ids.append(DstId(rid=rid, pnc=pid))
+    g.wait_ge(sem.adg, n_dg)
+    g.remote_dma_fused([
+        RemoteDMATransfer(dst_ids=ids, dma_engine_mask=m_all, remote_sem=sem.ard,
+                          srcs=[slot(T.Lnd, 4 + k)], dsts=[slot(T.Lnd, 4 + k) for d in order]),
+    ], local_sem=sem.snt)
+    sent[0] += len(_bits(m_all))
+    n_rd = len(order) * len(_bits(m_all))
+
+    Io = T.I[:, 16 * k:16 * (k + 1)]
     v.wait_ge(sem.gi, 4)
     vdone(v.tensor_scalar(T.XA[:, :], T.X[:, :], 15, None, A_.bitwise_and))
     vdone(v.tensor_scalar(T.XB[:, :], T.X[:, :], 3, 240, A_.logical_shift_right, A_.bitwise_and))
-    vdone(v.tensor_scalar(T.K2[:, :], T.I[:, 16 * k:16 * (k + 1)], 768, None, A_.bitwise_and))
+    vdone(v.tensor_scalar(T.K2[:, :], Io, 768, None, A_.bitwise_and))
+    vdone(v.tensor_scalar(T.U2[:, :], Io, 255, None, A_.bitwise_and))
+    vdone(v.tensor_scalar(T.Hh[:, :], Io, 10, None, A_.logical_shift_right))
     vsync()
     vdone(v.tensor_tensor(T.TP[:, :], T.XA[:, :], T.XB[:, :], A_.add))
+    vdone(v.tensor_scalar(T.Eq[:, :], T.Hh[:, :], h_far, None, A_.is_equal))
     vsync()
-    vdone(v.tensor_tensor(T.S2[:, :], T.K2[:, :], T.TP[:, :], A_.add))
+    vdone(v.tensor_tensor(T.D1[:, :], T.U2[:, :], T.TP[:, :], A_.subtract))
+    vdone(v.tensor_tensor(T.B2[:, :], T.K2[:, :], T.TP[:, :], A_.add))
+    vsync()
+    vdone(v.tensor_scalar(T.D2[:, :], T.D1[:, :], 4 * C, None, A_.add))
+    vsync()
+    vdone(v.tensor_tensor(T.M2[:, :], T.D2[:, :], T.Eq[:, :], A_.mult))
+    vsync()
+    vdone(v.tensor_tensor(T.S2[:, :], T.B2[:, :], T.M2[:, :], A_.add))
     vsync()
     vdone(v.tensor_copy(T.OFF2[:, :], T.S2[:, :]))
     vsync()
 
     v.wait_ge(sem.tl, nsib)
     v.wait_ge(sem.atl, n_tl)
-    v.tensor_copy(T.Y[:, :], T.Lnd[:, 0:4 * C].indirect(T.OFF2[:, 0:16])).then_inc(sem.yd, 1)
+    v.wait_ge(sem.adg, n_dg)
+    v.wait_ge(sem.ard, n_rd)
+    v.tensor_copy(T.Y[:, :], T.Lnd[:, 0:8 * C].indirect(T.OFF2[:, 0:16])).then_inc(sem.yd, 1)
     g.sync.wait_ge(sem.yd, 1)
     g.sync.dma_start(T.y[:, :], T.Y[:, :]).then_inc(sem.st, 16)
 
-    g.wait_ge(sem.snt, sent)
-    g.wait_ge(sem.asw, len(m_sw))
-    g.wait_ge(sem.acb, len(m_cb))
-    g.wait_ge(sem.adg, n_dg)
+    g.wait_ge(sem.snt, sent[0])
+    g.wait_ge(sem.asw, n_sw)
+    g.wait_ge(sem.acb, n_cb)
     g.wait_ge(sem.atl, n_tl)
+    g.wait_ge(sem.ard, n_rd)
     g.wait_ge(sem.st, 16)

from concourse.bass import DstId, RemoteDMATransfer
from concourse.mybir import AluOpType

SCRATCH = {
    "A": ("sbuf", [128, 1024], "bfloat16"),
    "S": ("sbuf", [128, 1024], "bfloat16"),
    "Lnd": ("sbuf", [128, 2048], "bfloat16"),
    "Y": ("sbuf", [128, 256], "bfloat16"),
    "G": ("sbuf", [128, 32], "int32"),
    "OFFG": ("sbuf", [128, 32], "uint16"),
    "IV": ("sbuf", [128, 512], "int32"),
    "VAL": ("sbuf", [128, 512], "int32"),
    "W": ("sbuf", [128, 4096], "float32"),
    "IL": ("sbuf", [128, 128], "int32"),
    "IL2": ("sbuf", [128, 128], "int32"),
    "L": ("sbuf", [128, 128], "float32"),
    "IM": ("sbuf", [128, 64], "int32"),
    "IM2": ("sbuf", [128, 64], "int32"),
    "Mask": ("sbuf", [128, 64], "float32"),
    "R": ("sbuf", [128, 64], "float32"),
    "I": ("sbuf", [128, 64], "int32"),
    "Hq": ("sbuf", [128, 64], "int32"),
    "U": ("sbuf", [128, 64], "int32"),
    "S1": ("sbuf", [128, 64], "int32"),
    "OFF1": ("sbuf", [128, 64], "uint16"),
    "X": ("sbuf", [128, 16], "int32"),
    "XA": ("sbuf", [128, 16], "int32"),
    "XB": ("sbuf", [128, 16], "int32"),
    "TP": ("sbuf", [128, 16], "int32"),
    "K2": ("sbuf", [128, 16], "int32"),
    "U2": ("sbuf", [128, 16], "int32"),
    "Hh": ("sbuf", [128, 16], "int32"),
    "Eq": ("sbuf", [128, 16], "int32"),
    "D1": ("sbuf", [128, 16], "int32"),
    "D2": ("sbuf", [128, 16], "int32"),
    "M2": ("sbuf", [128, 16], "int32"),
    "B2": ("sbuf", [128, 16], "int32"),
    "S2": ("sbuf", [128, 16], "int32"),
    "OFF2": ("sbuf", [128, 16], "uint16"),
    "P1": ("psum", [128, 512], "float32"),
    "P2": ("psum", [128, 512], "float32"),
}
SEMAPHORES = ["xl", "gl", "gi", "vs", "ts", "tl", "yd", "st", "asw", "acb", "adg", "atl", "ard", "snt"]

C = 256


def _bits(mask):
    return [e for e in range(16) if (mask >> e) & 1]


def rank_program(g, core, T, topo):
    rank = T.rank_of(core)
    if rank is None:
        return
    cores = list(T.cores)
    sem = T.sem
    A_ = AluOpType

    def place(c):
        return (topo.host(c), topo.chip(c))
    groups = []
    for c in cores:
        if place(c) not in groups:
            groups.append(place(c))
    members = [[c for c in cores if place(c) == gp] for gp in groups]
    h = groups.index(place(core))
    k = members[h].index(core)
    nsib = len(members[h])
    assert len(groups) == 4 and nsib == 4 and rank == 4 * h + k
    h_sw = h_cb = h_far = None
    for hh in range(4):
        if hh == h:
            continue
        peer = members[hh][k]
        if not topo.may_write(core, peer):
            h_far = hh
        elif topo.same_plane(core, peer):
            h_sw = hh
        else:
            h_cb = hh
    assert h_sw is not None and h_cb is not None and h_far is not None

    def slot(buf, n):
        return buf[:, C * n:C * (n + 1)]

    sent = [0]

    def send(to, out, in_, rsem):
        rid, pid = topo.addr(to, core)
        m = topo.mask(core, to)
        g.remote_dma(out, in_, rsem, sem.snt, pid, rid, m)
        sent[0] += len(_bits(m))
        return len(_bits(m))

    v, te = g.vector, g.tensor
    nv = [0]

    def vdone(ins):
        ins.then_inc(sem.vs, 1)
        nv[0] += 1

    def vsync():
        if nv[0]:
            v.wait_ge(sem.vs, nv[0])

    g.sync.dma_start(slot(T.A, h), T.x[:, :]).then_inc(sem.xl, 16)
    g.scalar.dma_start(T.G[:, :], T.goes[:, :]).then_inc(sem.gl, 16)

    g.iota(T.IV[:, :], [[128, 32], [8, 2], [4096, 8]], 0, 1).then_inc(sem.gi, 1)
    g.iota(T.IL[:, :], [[-1, 128]], 128, 1).then_inc(sem.gi, 1)
    g.iota(T.IM[:, :], [[0, 8], [-16, 8]], 128, 1).then_inc(sem.gi, 1)

    p_sw, p_cb = members[h_sw][k], members[h_cb][k]
    g.wait_ge(sem.xl, 16)
    if k % 2 == 0:
        n_sw = send(p_sw, slot(T.A, h), slot(T.A, h), sem.asw)
        n_cb = send(p_cb, slot(T.A, h), slot(T.A, h), sem.acb)
    else:
        n_cb = send(p_cb, slot(T.A, h), slot(T.A, h), sem.acb)
        n_sw = send(p_sw, slot(T.A, h), slot(T.A, h), sem.asw)
    g.iota(T.X[:, :], [[128, 16]], 0, 1).then_inc(sem.gi, 1)

    if k % 2 == 0:
        g.wait_ge(sem.asw, n_sw)
        n_dg = send(p_cb, slot(T.Lnd, 4 + k), slot(T.A, h_sw), sem.adg)
    else:
        g.wait_ge(sem.acb, n_cb)
        n_dg = send(p_sw, slot(T.Lnd, 4 + k), slot(T.A, h_cb), sem.adg)

    base = 4 * C * h
    vdone(v.memset(T.W[:, base:base + 4 * C], 0.0))
    vdone(v.memset(slot(T.A, h_far), 0.0))
    v.wait_ge(sem.gi, 3)
    vdone(v.tensor_scalar(T.VAL[:, :], T.IV[:, :], 3, None, A_.logical_shift_right))
    vdone(v.tensor_scalar(T.IL2[:, :], T.IL[:, :], 15, None, A_.bitwise_and))
    vdone(v.tensor_scalar(T.IM2[:, :], T.IM[:, :], 4, None, A_.logical_shift_right))
    vsync()
    vdone(v.tensor_scalar(T.L[:, :], T.IL2[:, :], 0, None, A_.is_equal))
    vdone(v.tensor_scalar(T.Mask[:, :], T.IM2[:, :], 8, None, A_.is_equal))
    v.wait_ge(sem.gl, 16)
    vdone(v.tensor_copy(T.OFFG[:, :], T.G[:, :]))
    vsync()
    vdone(v.tensor_copy(T.W[:, 0:4096].indirect(T.OFFG[:, 0:32]), T.VAL[:, :]))
    te.wait_ge(sem.vs, nv[0])
    for b in range(8):
        te.matmul(T.P1[:, 8 * b:8 * b + 8], T.W[:, base + 128 * b:base + 128 * (b + 1)], T.L[:, 0:8],
                  True, True).then_inc(sem.ts, 1)
    v.wait_ge(sem.ts, 8)
    vdone(v.tensor_tensor(T.R[:, :], T.P1[:, 0:64], T.Mask[:, :], A_.mult))
    te.wait_ge(sem.vs, nv[0])
    te.matmul(T.P2[:, 0:64], T.L[:, :], T.R[:, :], True, True).then_inc(sem.ts, 1)
    v.wait_ge(sem.ts, 9)
    vdone(v.tensor_copy(T.I[:, :], T.P2[:, 0:64]))
    vsync()
    vdone(v.tensor_scalar(T.Hq[:, :], T.I[:, :], 2, 768, A_.logical_shift_right, A_.bitwise_and))
    vdone(v.tensor_scalar(T.U[:, :], T.I[:, :], 255, None, A_.bitwise_and))
    vsync()
    vdone(v.tensor_tensor(T.S1[:, :], T.Hq[:, :], T.U[:, :], A_.add))
    vsync()
    vdone(v.tensor_copy(T.OFF1[:, :], T.S1[:, :]))
    vsync()

    v.wait_ge(sem.xl, 16)
    v.wait_ge(sem.asw, n_sw)
    v.wait_ge(sem.acb, n_cb)
    order = [(k + j) % nsib for j in range(1, nsib)]
    n_tl = 0
    for n, d in enumerate(order):
        v.tensor_copy(slot(T.S, d), T.A[:, 0:4 * C].indirect(T.OFF1[:, 16 * d:16 * (d + 1)])).then_inc(sem.tl, 1)
        g.wait_ge(sem.tl, n + 1)
        n_tl += send(members[h][d], slot(T.Lnd, k), slot(T.S, d), sem.atl)
    v.tensor_copy(slot(T.Lnd, k), T.A[:, 0:4 * C].indirect(T.OFF1[:, 16 * k:16 * (k + 1)])).then_inc(sem.tl, 1)

    m_all = topo.mask(core, members[h][order[0]])
    ids = []
    for d in order:
        m_all &= topo.mask(core, members[h][d])
        rid, pid = topo.addr(members[h][d], core)
        ids.append(DstId(rid=rid, pnc=pid))
    g.wait_ge(sem.adg, n_dg)
    g.remote_dma_fused([
        RemoteDMATransfer(dst_ids=ids, dma_engine_mask=m_all, remote_sem=sem.ard,
                          srcs=[slot(T.Lnd, 4 + k)], dsts=[slot(T.Lnd, 4 + k) for d in order]),
    ], local_sem=sem.snt)
    sent[0] += len(_bits(m_all))
    n_rd = len(order) * len(_bits(m_all))

    Io = T.I[:, 16 * k:16 * (k + 1)]
    v.wait_ge(sem.gi, 4)
    vdone(v.tensor_scalar(T.XA[:, :], T.X[:, :], 15, None, A_.bitwise_and))
    vdone(v.tensor_scalar(T.XB[:, :], T.X[:, :], 3, 240, A_.logical_shift_right, A_.bitwise_and))
    vdone(v.tensor_scalar(T.K2[:, :], Io, 768, None, A_.bitwise_and))
    vdone(v.tensor_scalar(T.U2[:, :], Io, 255, None, A_.bitwise_and))
    vdone(v.tensor_scalar(T.Hh[:, :], Io, 10, None, A_.logical_shift_right))
    vsync()
    vdone(v.tensor_tensor(T.TP[:, :], T.XA[:, :], T.XB[:, :], A_.add))
    vdone(v.tensor_scalar(T.Eq[:, :], T.Hh[:, :], h_far, None, A_.is_equal))
    vsync()
    vdone(v.tensor_tensor(T.D1[:, :], T.U2[:, :], T.TP[:, :], A_.subtract))
    vdone(v.tensor_tensor(T.B2[:, :], T.K2[:, :], T.TP[:, :], A_.add))
    vsync()
    vdone(v.tensor_scalar(T.D2[:, :], T.D1[:, :], 4 * C, None, A_.add))
    vsync()
    vdone(v.tensor_tensor(T.M2[:, :], T.D2[:, :], T.Eq[:, :], A_.mult))
    vsync()
    vdone(v.tensor_tensor(T.S2[:, :], T.B2[:, :], T.M2[:, :], A_.add))
    vsync()
    vdone(v.tensor_copy(T.OFF2[:, :], T.S2[:, :]))
    vsync()

    v.wait_ge(sem.tl, nsib)
    v.wait_ge(sem.atl, n_tl)
    v.wait_ge(sem.adg, n_dg)
    v.wait_ge(sem.ard, n_rd)
    v.tensor_copy(T.Y[:, :], T.Lnd[:, 0:8 * C].indirect(T.OFF2[:, 0:16])).then_inc(sem.yd, 1)
    g.sync.wait_ge(sem.yd, 1)
    g.sync.dma_start(T.y[:, :], T.Y[:, :]).then_inc(sem.st, 16)

    g.wait_ge(sem.snt, sent[0])
    g.wait_ge(sem.asw, n_sw)
    g.wait_ge(sem.acb, n_cb)
    g.wait_ge(sem.atl, n_tl)
    g.wait_ge(sem.ard, n_rd)
    g.wait_ge(sem.st, 16)
